import numpy as np
import ml_dtypes


def mxq(x, axis, fmt="e4m3"):
    dtype, down = {"e4m3": (ml_dtypes.float8_e4m3fn, 7), "e5m2": (ml_dtypes.float8_e5m2, 14)}[fmt]
    v = np.moveaxis(np.asarray(x, np.float32).astype(ml_dtypes.bfloat16).astype(np.float64), axis, -1)
    blocks = v.reshape(v.shape[:-1] + (-1, 32))
    amax = np.abs(blocks).max(-1, keepdims=True)
    byte = np.maximum(np.where(amax > 0, np.frexp(amax)[1] - 1 + 127, 0) - down, 1)
    scale = np.exp2(byte - 127.0)
    codes = (blocks / scale).astype(np.float32).astype(dtype).astype(np.float64)
    return np.moveaxis((codes * scale).reshape(v.shape), -1, axis)


WIDE = False


def mx_kscale(k):
    if not WIDE:
        return np.ones(k)
    levels = np.array([10, -10, 5, -5, 0])
    if k % 512:
        return np.exp2(np.random.permutation(np.resize(levels, k // 32))).repeat(32)
    a = np.empty((k // 512, 16))
    for p in range(k // 512):
        a[p, :8] = np.random.permutation(np.resize(levels, 8))
        for g in range(8):
            far = levels[np.abs(levels - a[p, g]) >= 10]
            a[p, g + 8] = far[np.random.randint(len(far))]
    return np.exp2(a.ravel()).repeat(32)


def f64(x):
    return np.asarray(x).astype(np.float64)


def striped(idx):
    return np.tile(idx.reshape(-1, 16).T, (8, 1)).astype(np.uint16)


def unstriped(offs):
    return offs[:16].T.reshape(-1).astype(np.int64)


E2M1 = np.array([0.0, 0.5, 1.0, 1.5, 2.0, 3.0, 4.0, 6.0, -0.0, -0.5, -1.0, -1.5, -2.0, -3.0, -4.0, -6.0])


def pack_weight(w, fmt):
    k, n = w.shape
    w = f64(np.asarray(w, np.float32).astype(ml_dtypes.bfloat16)).reshape(k // 32, 32, n)
    amax = np.abs(w).max(1)
    if fmt == "e4m3":
        byte = np.frexp(amax)[1] - 1 + 127 - 7
    else:
        mant, ex = np.frexp(amax / 6.0)
        byte = np.where(mant > 0.5, ex, ex - 1) + 127
    byte = np.clip(np.where(amax > 0, byte, 1), 1, 254)
    scaled = (w * np.exp2(127.0 - byte)[:, None, :]).reshape(k, n).astype(np.float32)
    by_word = np.ascontiguousarray(scaled.reshape(k // 512, 128, 4, n).transpose(0, 1, 3, 2))
    if fmt == "e4m3":
        words = by_word.astype(ml_dtypes.float8_e4m3fn).view(np.uint8)
    else:
        c = by_word.astype(ml_dtypes.float4_e2m1fn).view(np.uint8) & 0xF
        words = (c[..., 0::2] | (c[..., 1::2] << 4)).reshape(k // 512, 128, 2 * n)
    return np.ascontiguousarray(words), np.ascontiguousarray(byte.astype(np.uint8).reshape(k // 512, 16, n))


def unpack_weight(words, scales, fmt):
    g, _, n = scales.shape
    words = np.ascontiguousarray(words).reshape(g, 128, n, -1)
    if fmt == "e4m3":
        vals = words.view(ml_dtypes.float8_e4m3fn).astype(np.float64)
    else:
        nib = np.empty((g, 128, n, 4), np.uint8)
        nib[..., 0::2] = words & 0xF
        nib[..., 1::2] = words >> 4
        vals = E2M1[nib]
    vals = vals * np.repeat(np.exp2(scales.astype(np.float64) - 127.0), 8, axis=1)[..., None]
    return vals.transpose(0, 1, 3, 2).reshape(g * 512, n)


def gelu(v):
    return 0.5 * v * (1.0 + np.tanh(np.sqrt(2.0 / np.pi) * (v + 0.044715 * v**3)))


K, T, S, P, H, N = 1536, 2048, 1024, 512, 1024, 512

def setup_inputs():
    n = np.random.standard_normal
    s = mx_kscale(K)[:, None]
    u = mx_kscale(H)[:, None]
    tab_words, tab_scales = pack_weight(n((K, T)) * s, "e4m3")
    w5_words, w5_scales = pack_weight(n((H, N)) / np.sqrt(H) / u, "e2m1")
    return {
        "tab_words": tab_words, "tab_scales": tab_scales,
        "offs": striped(np.random.permutation(T)[:S]),
        "pos1": striped(np.random.permutation(S)[:P]),
        "pos2": striped(np.random.permutation(S)[:P]),
        "w1": (0.9 * n((K, H)) / np.sqrt(K) / s).astype(np.float32),
        "thr": n(H).astype(np.float32),
        "temp": np.random.uniform(0.4, 1.6, H).astype(np.float32),
        "sgn": (2.0 * n(H)).astype(np.float32),
        "gain": (np.random.uniform(0.6, 1.6, H) * u[:, 0]).astype(np.float32),
        "focus": (4.0 * n((H, P)) * u).astype(np.float32),
        "w4": (n((H, N)) / np.sqrt(H) / u).astype(np.float32),
        "w5_words": w5_words, "w5_scales": w5_scales,
        "bias": (0.4 * n(N)).astype(np.float32),
    }

def reference(tab_words, tab_scales, offs, pos1, pos2, w1, thr, temp, sgn, gain, focus, w4, w5_words, w5_scales, bias):
    v = unpack_weight(tab_words, tab_scales, "e4m3")[:, unstriped(offs)]
    h = mxq(f64(w1), 0, "e4m3").T @ v
    a = 1.0 / (1.0 + np.exp(-(h[:, unstriped(pos1)] + f64(thr)[:, None])))
    top = h.max(axis=1)
    c = np.exp(f64(temp)[:, None] * (h[:, unstriped(pos2)] - top[:, None]))
    diff = (a - f64(sgn)[:, None] * c) * f64(gain)[:, None]
    both = a * c * f64(focus)
    w5 = unpack_weight(w5_words, w5_scales, "e2m1")
    y = mxq(f64(w4), 0, "e4m3").T @ mxq(diff, 0, "e4m3") + w5.T @ mxq(both, 0, "e4m3")
    return y + f64(bias)[:, None]

@@ -1,0 +1,245 @@
+from contextlib import ExitStack
+
+import concourse.mybir as mybir
+
+K, T, S, M, H, N = 1536, 2048, 1024, 512, 1024, 512
+FLOPS = 2 * K * H * S + 2 * 2 * H * N * M
+
+F32 = mybir.dt.float32
+BF16 = mybir.dt.bfloat16
+I32 = mybir.dt.int32
+U32 = mybir.dt.uint32
+U16 = mybir.dt.uint16
+U8 = mybir.dt.uint8
+FP8X4 = mybir.dt.float8_e4m3fn_x4
+FP4X4 = mybir.dt.float4_e2m1fn_x4
+ACT = mybir.ActivationFunctionType
+ALU = mybir.AluOpType
+
+P = 128
+PACK = 4
+K_PASS = P * PACK
+K_PASSES = K // K_PASS
+R_PASSES = H // K_PASS
+BANK = 512
+HALF = M // 2
+
+
+def tile_list_burst_cancel_scores_kernel(
+    tc, tab_words, tab_scales, offs, pos1, pos2, w1, thr, temp, sgn, gain, focus, w4, w5_words, w5_scales, bias, out
+):
+    nc = tc.nc
+    with ExitStack() as ctx:
+        lists = ctx.enter_context(tc.tile_pool(name="lists", bufs=1))
+        keep = ctx.enter_context(tc.tile_pool(name="keep", bufs=1))
+        ring = ctx.enter_context(tc.tile_pool(name="ring", bufs=1))
+        psum = ctx.enter_context(tc.psum_pool(name="psum", bufs=1))
+
+        offs_sb = lists.tile([P, S // 16], U16, name="offs_sb")
+        pos1_sb = lists.tile([P, M // 16], U16, name="pos1_sb")
+        pos2_sb = lists.tile([P, M // 16], U16, name="pos2_sb")
+
+        def load_rows(src, name):
+            raw = ring.tile([P, PACK, 512], F32, name=name, tag="raw", bufs=7)
+            nc.sync.dma_start(out=raw[:], in_=src.rearrange("(p j) c -> p j c", j=PACK))
+            return raw
+
+        def load_table(a):
+            words = keep.tile([P, T], I32, name=f"tab{a}")
+            nc.sync.dma_start(out=words[:], in_=tab_words[a].rearrange("p t i -> p (t i)").bitcast(I32))
+            return words
+
+        def load_vector(vec, name):
+            col = keep.tile([P, R_PASSES, PACK], F32, name=name)
+            nc.sync.dma_start(out=col[:], in_=vec.rearrange("(b p t) -> p b t", p=P, t=PACK))
+            return col[:].rearrange("p b t -> p (b t)")
+
+        def w1_rows(a, b):
+            return w1[a * K_PASS : (a + 1) * K_PASS, b * 512 : (b + 1) * 512]
+
+        tab_planes = keep.tile([P, T], U8, name="tab_planes")
+        nc.gpsimd.memset(tab_planes[:].bitcast(I32), 0)
+        w5_planes = keep.tile([P, R_PASSES, N], U8, name="w5_planes", align_bytes=64)
+        nc.gpsimd.memset(w5_planes[:].rearrange("p a n -> p (a n)").bitcast(I32), 0)
+        tab = []
+        w1_raw = {}
+        tab.append(load_table(0))
+        nc.sync.dma_start(offs_sb[:], offs)
+        w1_raw[0, 0] = load_rows(w1_rows(0, 0), "w1raw00")
+        for q in range(4):
+            nc.sync.dma_start(
+                out=tab_planes[32 * q : 32 * q + 4 * K_PASSES, :].bitcast(I32),
+                in_=tab_scales[:, 4 * q : 4 * q + 4, :].bitcast(I32),
+            )
+        for a in range(1, K_PASSES):
+            tab.append(load_table(a))
+            w1_raw[a, 0] = load_rows(w1_rows(a, 0), f"w1raw{a}0")
+        w1_raw[0, 1] = load_rows(w1_rows(0, 1), "w1raw01")
+        nc.sync.dma_start(pos1_sb[:], pos1)
+        thr_sb = load_vector(thr, "thr_sb")
+        w1_raw[1, 1] = load_rows(w1_rows(1, 1), "w1raw11")
+        w1_raw[2, 1] = load_rows(w1_rows(2, 1), "w1raw21")
+        nc.sync.dma_start(pos2_sb[:], pos2)
+        temp_sb = load_vector(temp, "temp_sb")
+        gain_sb = load_vector(gain, "gain_sb")
+        sgn_sb = load_vector(sgn, "sgn_sb")
+        w4_raw = []
+        focus_sb = []
+        for b in range(R_PASSES):
+            rows = slice(b * K_PASS, (b + 1) * K_PASS)
+            w4_raw.append(load_rows(w4[rows, :], f"w4raw{b}"))
+            focus_sb.append(load_rows(focus[rows, :], f"focus{b}"))
+        w5_codes = keep.tile([P, R_PASSES, 2 * N], U8, name="w5_codes", align_bytes=64)
+        nc.sync.dma_start(out=w5_codes[:].bitcast(I32), in_=w5_words.rearrange("a p n -> p a n").bitcast(I32))
+        for q in range(4):
+            nc.sync.dma_start(
+                out=w5_planes[32 * q : 32 * q + 4, :, :].bitcast(I32),
+                in_=w5_scales[:, 4 * q : 4 * q + 4, :].rearrange("a q n -> q a n").bitcast(I32),
+            )
+        bias_sb = keep.tile([P, N // P], F32, name="bias_sb")
+        with nc.allow_non_contiguous_dma(reason="one bias value for each output row"):
+            nc.sync.dma_start(out=bias_sb[:], in_=bias.rearrange("(j p) -> p j", p=P))
+
+        def staging(name):
+            return ring.tile([P, 2048], BF16, name=name, tag="bf", bufs=4, align_bytes=64)
+
+        def quantize(grouped, name):
+            codes = keep.tile([P, 512], U32, name=name + "_codes", align_bytes=64)
+            planes = keep.tile([P, 512], U8, name=name + "_planes", align_bytes=64)
+            nc.vector.quantize_mx(out=codes[:].bitcast(FP8X4), scales=planes[:], in_=grouped[:])
+            return codes, planes
+
+        def round_w1(a, b):
+            grouped = staging(f"w1bf{a}{b}")
+            nc.scalar.copy(
+                out=grouped[:].rearrange("p (t m j) -> p m j t", t=PACK, j=PACK),
+                in_=w1_raw[a, b][:].rearrange("p j (m t) -> p m j t", t=PACK),
+            )
+            return grouped
+
+        def gather_words(a):
+            picked = keep.tile([P, S], U32, name=f"picked{a}", align_bytes=64)
+            nc.vector.tensor_copy(picked[:], tab[a][:].bitcast(U32).indirect(offs_sb[:]))
+            return picked
+
+        picked_planes = keep.tile([P, S], U8, name="picked_planes", align_bytes=64)
+        picked = []
+        peaks = keep.tile([P, 2, R_PASSES * PACK], F32, name="peaks")
+        h = {}
+        for b in range(R_PASSES):
+            banks = {}
+            for t in range(PACK):
+                for half in range(2):
+                    banks[t, half] = psum.tile([P, BANK], F32, name=f"h{b}{t}{half}", tag=f"bank{2 * t + half}")
+            for a in range(K_PASSES):
+                if b == 0:
+                    picked.append(gather_words(a))
+                    if a == 0:
+                        nc.vector.tensor_copy(picked_planes[:], tab_planes[:].indirect(offs_sb[:]))
+                codes, planes = quantize(round_w1(a, b), f"w1q{a}{b}")
+                for t in range(PACK):
+                    for half in range(2):
+                        cols = slice(half * BANK, (half + 1) * BANK)
+                        nc.tensor.matmul_mx(
+                            out=banks[t, half][:],
+                            lhsT=codes[:, t * P : (t + 1) * P].bitcast(FP8X4),
+                            lhsT_scale=planes[:, t * P : (t + 1) * P],
+                            rhs=picked[a][:, cols].bitcast(FP8X4),
+                            rhs_scale=picked_planes[4 * a : P, cols],
+                            start=(a == 0),
+                            stop=(a == K_PASSES - 1),
+                        )
+            for t in range(PACK):
+                h[b, t] = keep.tile([P, S], F32, name=f"hsb{b}{t}")
+                for half in range(2):
+                    nc.vector.tensor_scalar(
+                        out=h[b, t][:, half * BANK : (half + 1) * BANK],
+                        in0=banks[t, half][:],
+                        scalar1=1.0,
+                        scalar2=None,
+                        op0=ALU.mult,
+                        op1=ALU.max,
+                        accum_out=peaks[:, half, PACK * b + t : PACK * b + t + 1],
+                    )
+
+        burst = []
+        for b in range(R_PASSES):
+            burst.append(keep.tile([P, PACK, M], F32, name=f"burst{b}"))
+            for t in range(PACK):
+                r = PACK * b + t
+                nc.scalar.activation(
+                    out=burst[b][:, t, :], in_=h[b, t][:].indirect(pos1_sb[:]), func=ACT.Sigmoid, bias=thr_sb[:, r : r + 1]
+                )
+
+        top = keep.tile([P, R_PASSES * PACK], F32, name="top")
+        nc.vector.tensor_tensor(out=top[:], in0=peaks[:, 0, :], in1=peaks[:, 1, :], op=ALU.max)
+        exp_bias = keep.tile([P, R_PASSES * PACK], F32, name="exp_bias")
+        nc.vector.scalar_tensor_tensor(out=exp_bias[:], in0=top[:], scalar=-1.0, in1=temp_sb, op0=ALU.mult, op1=ALU.mult)
+        cancel_gain = keep.tile([P, R_PASSES * PACK], F32, name="cancel_gain")
+        nc.vector.scalar_tensor_tensor(out=cancel_gain[:], in0=sgn_sb, scalar=-1.0, in1=gain_sb, op0=ALU.mult, op1=ALU.mult)
+
+        w4_q = []
+        for b in range(R_PASSES):
+            nc.vector.tensor_tensor(out=focus_sb[b][:], in0=burst[b][:], in1=focus_sb[b][:], op=ALU.mult)
+            for t in range(PACK):
+                r = PACK * b + t
+                nc.vector.tensor_scalar_mul(out=burst[b][:, t, :], in0=burst[b][:, t, :], scalar1=gain_sb[:, r : r + 1])
+            grouped = staging(f"w4bf{b}")
+            nc.vector.tensor_copy(
+                out=grouped[:].rearrange("p (c i j) -> p c j i", i=4, j=PACK),
+                in_=w4_raw[b][:].rearrange("p j (c i) -> p c j i", i=4),
+            )
+            w4_q.append(quantize(grouped, f"w4q{b}"))
+
+        def walk(planes):
+            return planes.rearrange("p t (c i) -> p c t i", i=4)
+
+        for half in range(2):
+            cols = slice(half * HALF, (half + 1) * HALF)
+            sums = [psum.tile([P, HALF], F32, name=f"y{j}{half}", tag=f"bank{2 * j + half}") for j in range(N // P)]
+            for b in range(R_PASSES):
+                cancel = ring.tile([P, PACK, HALF], F32, name=f"cancel{b}{half}", tag="cancel", bufs=3)
+                share = ring.tile([P, PACK, HALF], F32, name=f"share{b}{half}", tag="share", bufs=2)
+                for t in range(PACK):
+                    r = PACK * b + t
+                    nc.scalar.activation(
+                        out=cancel[:, t, :],
+                        in_=h[b, t][:].indirect(pos2_sb[:, half * (HALF // 16) : (half + 1) * (HALF // 16)]),
+                        func=ACT.Exp,
+                        bias=exp_bias[:, r : r + 1],
+                        scale=temp_sb[:, r : r + 1],
+                    )
+                for t in range(PACK):
+                    r = PACK * b + t
+                    nc.scalar.activation(out=share[:, t, :], in_=cancel[:, t, :], func=ACT.Copy, scale=cancel_gain[:, r : r + 1])
+                grouped = staging(f"feat{b}{half}")
+                woven = grouped[:].rearrange("p (f c i t) -> p f c t i", f=2, i=4, t=PACK)
+                nc.vector.tensor_tensor(out=woven[:, 1], in0=walk(cancel[:]), in1=walk(focus_sb[b][:, :, cols]), op=ALU.mult)
+                nc.vector.tensor_tensor(out=woven[:, 0], in0=walk(share[:]), in1=walk(burst[b][:, :, cols]), op=ALU.add)
+                codes, planes = quantize(grouped, f"featq{b}{half}")
+                for j in range(N // P):
+                    nc.tensor.matmul_mx(
+                        out=sums[j][:],
+                        lhsT=w4_q[b][0][:, j * P : (j + 1) * P].bitcast(FP8X4),
+                        lhsT_scale=w4_q[b][1][:, j * P : (j + 1) * P],
+                        rhs=codes[:, 0:HALF].bitcast(FP8X4),
+                        rhs_scale=planes[:, 0:HALF],
+                        start=(b == 0),
+                        stop=False,
+                    )
+                    nc.tensor.matmul_mx(
+                        out=sums[j][:],
+                        lhsT=w5_codes[:, b, 2 * j * P : 2 * (j + 1) * P].bitcast(FP4X4),
+                        lhsT_scale=w5_planes[:, b, j * P : (j + 1) * P],
+                        rhs=codes[:, HALF:M].bitcast(FP8X4),
+                        rhs_scale=planes[:, HALF:M],
+                        start=False,
+                        stop=(b == R_PASSES - 1),
+                    )
+            for j in range(N // P):
+                result = ring.tile([P, HALF], F32, name=f"out{j}{half}", tag="result", bufs=8)
+                if half == 1 and j % 2 == 1:
+                    nc.scalar.activation(out=result[:], in_=sums[j][:], func=ACT.Identity, bias=bias_sb[:, j : j + 1])
+                else:
+                    nc.vector.tensor_scalar_add(out=result[:], in0=sums[j][:], scalar1=bias_sb[:, j : j + 1])
+                nc.sync.dma_start(out=out[j * P : (j + 1) * P, cols], in_=result[:])

@@ -23,6 +23,8 @@ K_PASSES = K // K_PASS
 R_PASSES = H // K_PASS
 BANK = 512
 HALF = M // 2
+GPSIMD_W1 = ()
+GPSIMD_W4 = False
 
 
 def tile_list_burst_cancel_scores_kernel(
@@ -40,7 +42,7 @@ def tile_list_burst_cancel_scores_kernel(
         pos2_sb = lists.tile([P, M // 16], U16, name="pos2_sb")
 
         def load_rows(src, name):
-            raw = ring.tile([P, PACK, 512], F32, name=name, tag="raw", bufs=7)
+            raw = ring.tile([P, PACK, 512], F32, name=name, tag="raw", bufs=5)
             nc.sync.dma_start(out=raw[:], in_=src.rearrange("(p j) c -> p j c", j=PACK))
             return raw
 
@@ -73,22 +75,25 @@ def tile_list_burst_cancel_scores_kernel(
             )
         for a in range(1, K_PASSES):
             tab.append(load_table(a))
-            w1_raw[a, 0] = load_rows(w1_rows(a, 0), f"w1raw{a}0")
+            if a < K_PASSES - 1:
+                w1_raw[a, 0] = load_rows(w1_rows(a, 0), f"w1raw{a}0")
+        last_halves = []
+        for half in range(2):
+            part = keep.tile([P, PACK, 256], F32, name=f"w1last{half}")
+            src = w1[(K_PASSES - 1) * K_PASS :, half * 256 : (half + 1) * 256]
+            nc.sync.dma_start(out=part[:], in_=src.rearrange("(p j) c -> p j c", j=PACK))
+            last_halves.append(part)
         w1_raw[0, 1] = load_rows(w1_rows(0, 1), "w1raw01")
-        nc.sync.dma_start(pos1_sb[:], pos1)
-        thr_sb = load_vector(thr, "thr_sb")
         w1_raw[1, 1] = load_rows(w1_rows(1, 1), "w1raw11")
         w1_raw[2, 1] = load_rows(w1_rows(2, 1), "w1raw21")
+        nc.sync.dma_start(pos1_sb[:], pos1)
+        thr_sb = load_vector(thr, "thr_sb")
         nc.sync.dma_start(pos2_sb[:], pos2)
         temp_sb = load_vector(temp, "temp_sb")
         gain_sb = load_vector(gain, "gain_sb")
         sgn_sb = load_vector(sgn, "sgn_sb")
-        w4_raw = []
-        focus_sb = []
-        for b in range(R_PASSES):
-            rows = slice(b * K_PASS, (b + 1) * K_PASS)
-            w4_raw.append(load_rows(w4[rows, :], f"w4raw{b}"))
-            focus_sb.append(load_rows(focus[rows, :], f"focus{b}"))
+        focus_sb = [load_rows(focus[b * K_PASS : (b + 1) * K_PASS, :], f"focus{b}") for b in range(R_PASSES)]
+        w4_raw = [load_rows(w4[b * K_PASS : (b + 1) * K_PASS, :], f"w4raw{b}") for b in range(R_PASSES)]
         w5_codes = keep.tile([P, R_PASSES, 2 * N], U8, name="w5_codes", align_bytes=64)
         nc.sync.dma_start(out=w5_codes[:].bitcast(I32), in_=w5_words.rearrange("a p n -> p a n").bitcast(I32))
         for q in range(4):
@@ -101,20 +106,35 @@ def tile_list_burst_cancel_scores_kernel(
             nc.sync.dma_start(out=bias_sb[:], in_=bias.rearrange("(j p) -> p j", p=P))
 
         def staging(name):
-            return ring.tile([P, 2048], BF16, name=name, tag="bf", bufs=4, align_bytes=64)
+            return ring.tile([P, 2048], BF16, name=name, tag="bf", bufs=2, align_bytes=64)
 
         def quantize(grouped, name):
-            codes = keep.tile([P, 512], U32, name=name + "_codes", align_bytes=64)
-            planes = keep.tile([P, 512], U8, name=name + "_planes", align_bytes=64)
+            width = grouped.shape[1] // PACK
+            codes = keep.tile([P, width], U32, name=name + "_codes", align_bytes=64)
+            planes = keep.tile([P, width], U8, name=name + "_planes", align_bytes=64)
             nc.vector.quantize_mx(out=codes[:].bitcast(FP8X4), scales=planes[:], in_=grouped[:])
             return codes, planes
 
         def round_w1(a, b):
-            grouped = staging(f"w1bf{a}{b}")
-            nc.scalar.copy(
-                out=grouped[:].rearrange("p (t m j) -> p m j t", t=PACK, j=PACK),
-                in_=w1_raw[a, b][:].rearrange("p j (m t) -> p m j t", t=PACK),
-            )
+            if (a, b) == (1, 1):
+                grouped = ring.tile([P, 2048], BF16, name="w1bf11", tag="handover", bufs=1, align_bytes=64)
+            else:
+                grouped = staging(f"w1bf{a}{b}")
+            dealt = grouped[:].rearrange("p (t m j) -> p m j t", t=PACK, j=PACK)
+            if (a, b) == (K_PASSES - 1, 0):
+                nc.scalar.copy(out=dealt[:, 0:64], in_=last_halves[0][:].rearrange("p j (m t) -> p m j t", t=PACK))
+                nc.scalar.copy(out=dealt[:, 64:128], in_=last_halves[1][:].rearrange("p j (m t) -> p m j t", t=PACK))
+            elif (a, b) == (K_PASSES - 1, 1):
+                natural = w1_raw[a, b][:].rearrange("p j (m t) -> p m j t", t=PACK)
+                nc.vector.tensor_copy(out=dealt[:, 0:64], in_=natural[:, 0:64])
+                nc.scalar.copy(out=dealt[:, 64:128], in_=natural[:, 64:128])
+            elif (a, b) in GPSIMD_W1:
+                nc.gpsimd.tensor_scalar(
+                    out=dealt, in0=w1_raw[a, b][:].rearrange("p j (m t) -> p m j t", t=PACK),
+                    scalar1=1.0, scalar2=0.0, op0=ALU.mult, op1=ALU.add,
+                )
+            else:
+                nc.scalar.copy(out=dealt, in_=w1_raw[a, b][:].rearrange("p j (m t) -> p m j t", t=PACK))
             return grouped
 
         def gather_words(a):
@@ -126,18 +146,15 @@ def tile_list_burst_cancel_scores_kernel(
         picked = []
         peaks = keep.tile([P, 2, R_PASSES * PACK], F32, name="peaks")
         h = {}
-        for b in range(R_PASSES):
+        w1_q = {}
+
+        def multiply(b):
             banks = {}
             for t in range(PACK):
                 for half in range(2):
                     banks[t, half] = psum.tile([P, BANK], F32, name=f"h{b}{t}{half}", tag=f"bank{2 * t + half}")
-            for a in range(K_PASSES):
-                if b == 0:
-                    picked.append(gather_words(a))
-                    if a == 0:
-                        nc.vector.tensor_copy(picked_planes[:], tab_planes[:].indirect(offs_sb[:]))
-                codes, planes = quantize(round_w1(a, b), f"w1q{a}{b}")
-                for t in range(PACK):
+                for a in range(K_PASSES):
+                    codes, planes = w1_q[a, b]
                     for half in range(2):
                         cols = slice(half * BANK, (half + 1) * BANK)
                         nc.tensor.matmul_mx(
@@ -149,8 +166,14 @@ def tile_list_burst_cancel_scores_kernel(
                             start=(a == 0),
                             stop=(a == K_PASSES - 1),
                         )
+            return banks
+
+        def empty(b, banks):
             for t in range(PACK):
-                h[b, t] = keep.tile([P, S], F32, name=f"hsb{b}{t}")
+                if (b, t) == (0, PACK - 1):
+                    h[b, t] = ring.tile([P, S], F32, name="hsb03", tag="handover", bufs=1, align_bytes=64)
+                else:
+                    h[b, t] = keep.tile([P, S], F32, name=f"hsb{b}{t}")
                 for half in range(2):
                     nc.vector.tensor_scalar(
                         out=h[b, t][:, half * BANK : (half + 1) * BANK],
@@ -161,6 +184,17 @@ def tile_list_burst_cancel_scores_kernel(
                         op1=ALU.max,
                         accum_out=peaks[:, half, PACK * b + t : PACK * b + t + 1],
                     )
+
+        for a in range(K_PASSES):
+            picked.append(gather_words(a))
+            if a == 0:
+                nc.vector.tensor_copy(picked_planes[:], tab_planes[:].indirect(offs_sb[:]))
+            w1_q[a, 0] = quantize(round_w1(a, 0), f"w1q{a}0")
+        banks = multiply(0)
+        for a in range(K_PASSES):
+            w1_q[a, 1] = quantize(round_w1(a, 1), f"w1q{a}1")
+        empty(0, banks)
+        empty(1, multiply(1))
 
         burst = []
         for b in range(R_PASSES):
@@ -180,26 +214,38 @@ def tile_list_burst_cancel_scores_kernel(
 
         w4_q = []
         for b in range(R_PASSES):
-            nc.vector.tensor_tensor(out=focus_sb[b][:], in0=burst[b][:], in1=focus_sb[b][:], op=ALU.mult)
+            for t in range(PACK):
+                nc.vector.tensor_tensor(out=focus_sb[b][:, t, :], in0=burst[b][:, t, :], in1=focus_sb[b][:, t, :], op=ALU.mult)
             for t in range(PACK):
                 r = PACK * b + t
                 nc.vector.tensor_scalar_mul(out=burst[b][:, t, :], in0=burst[b][:, t, :], scalar1=gain_sb[:, r : r + 1])
+
+        def prepare_w4(b):
             grouped = staging(f"w4bf{b}")
-            nc.vector.tensor_copy(
-                out=grouped[:].rearrange("p (c i j) -> p c j i", i=4, j=PACK),
-                in_=w4_raw[b][:].rearrange("p j (c i) -> p c j i", i=4),
-            )
+            w4_out = grouped[:].rearrange("p (c i j) -> p c j i", i=4, j=PACK)
+            w4_in = w4_raw[b][:].rearrange("p j (c i) -> p c j i", i=4)
+            if GPSIMD_W4:
+                nc.gpsimd.tensor_scalar(out=w4_out, in0=w4_in, scalar1=1.0, scalar2=0.0, op0=ALU.mult, op1=ALU.add)
+            else:
+                nc.vector.tensor_copy(out=w4_out, in_=w4_in)
             w4_q.append(quantize(grouped, f"w4q{b}"))
+
+        for b in range(R_PASSES):
+            prepare_w4(b)
 
         def walk(planes):
             return planes.rearrange("p t (c i) -> p c t i", i=4)
 
+        def weave(grouped):
+            return grouped[:].rearrange("p (c i t) -> p c t i", i=4, t=PACK)
+
+        sums = []
         for half in range(2):
             cols = slice(half * HALF, (half + 1) * HALF)
-            sums = [psum.tile([P, HALF], F32, name=f"y{j}{half}", tag=f"bank{2 * j + half}") for j in range(N // P)]
+            sums.append([psum.tile([P, HALF], F32, name=f"y{j}{half}", tag=f"bank{2 * j + half}") for j in range(N // P)])
             for b in range(R_PASSES):
-                cancel = ring.tile([P, PACK, HALF], F32, name=f"cancel{b}{half}", tag="cancel", bufs=3)
-                share = ring.tile([P, PACK, HALF], F32, name=f"share{b}{half}", tag="share", bufs=2)
+                cancel = ring.tile([P, PACK, HALF], F32, name=f"cancel{b}{half}", tag="cancel", bufs=4)
+                share = ring.tile([P, PACK, HALF], F32, name=f"share{b}{half}", tag="share", bufs=4)
                 for t in range(PACK):
                     r = PACK * b + t
                     nc.scalar.activation(
@@ -212,34 +258,39 @@ def tile_list_burst_cancel_scores_kernel(
                 for t in range(PACK):
                     r = PACK * b + t
                     nc.scalar.activation(out=share[:, t, :], in_=cancel[:, t, :], func=ACT.Copy, scale=cancel_gain[:, r : r + 1])
-                grouped = staging(f"feat{b}{half}")
-                woven = grouped[:].rearrange("p (f c i t) -> p f c t i", f=2, i=4, t=PACK)
-                nc.vector.tensor_tensor(out=woven[:, 1], in0=walk(cancel[:]), in1=walk(focus_sb[b][:, :, cols]), op=ALU.mult)
-                nc.vector.tensor_tensor(out=woven[:, 0], in0=walk(share[:]), in1=walk(burst[b][:, :, cols]), op=ALU.add)
-                codes, planes = quantize(grouped, f"featq{b}{half}")
-                for j in range(N // P):
-                    nc.tensor.matmul_mx(
-                        out=sums[j][:],
-                        lhsT=w4_q[b][0][:, j * P : (j + 1) * P].bitcast(FP8X4),
-                        lhsT_scale=w4_q[b][1][:, j * P : (j + 1) * P],
-                        rhs=codes[:, 0:HALF].bitcast(FP8X4),
-                        rhs_scale=planes[:, 0:HALF],
-                        start=(b == 0),
-                        stop=False,
-                    )
-                    nc.tensor.matmul_mx(
-                        out=sums[j][:],
-                        lhsT=w5_codes[:, b, 2 * j * P : 2 * (j + 1) * P].bitcast(FP4X4),
-                        lhsT_scale=w5_planes[:, b, j * P : (j + 1) * P],
-                        rhs=codes[:, HALF:M].bitcast(FP8X4),
-                        rhs_scale=planes[:, HALF:M],
-                        start=False,
-                        stop=(b == R_PASSES - 1),
-                    )
+                last = half == 1 and b == R_PASSES - 1
+                width = HALF // 2 if last else HALF
+                pieces = range(0, HALF, width)
+                for first, second, op, name in ((cancel, focus_sb[b], ALU.mult, "both"), (share, burst[b], ALU.add, "diff")):
+                    for c0 in pieces:
+                        feat = ring.tile([P, PACK * width], BF16, name=f"{name}{b}{half}{c0}", tag="feat", bufs=4, align_bytes=64)
+                        wide = slice(half * HALF + c0, half * HALF + c0 + width)
+                        nc.vector.tensor_tensor(
+                            out=weave(feat), in0=walk(first[:, :, c0 : c0 + width]), in1=walk(second[:, :, wide]), op=op
+                        )
+                        codes, planes = quantize(feat, f"{name}q{b}{half}{c0}")
+                        for j in range(N // P):
+                            if name == "both":
+                                weight = w5_codes[:, b, 2 * j * P : 2 * (j + 1) * P].bitcast(FP4X4)
+                                weight_planes = w5_planes[:, b, j * P : (j + 1) * P]
+                            else:
+                                weight = w4_q[b][0][:, j * P : (j + 1) * P].bitcast(FP8X4)
+                                weight_planes = w4_q[b][1][:, j * P : (j + 1) * P]
+                            nc.tensor.matmul_mx(
+                                out=sums[half][j][:, c0 : c0 + width],
+                                lhsT=weight,
+                                lhsT_scale=weight_planes,
+                                rhs=codes[:].bitcast(FP8X4),
+                                rhs_scale=planes[:],
+                                start=(b == 0 and name == "both"),
+                                stop=(b == R_PASSES - 1 and name == "diff" and c0 == pieces[-1]),
+                            )
+        for half in range(2):
+            cols = slice(half * HALF, (half + 1) * HALF)
             for j in range(N // P):
                 result = ring.tile([P, HALF], F32, name=f"out{j}{half}", tag="result", bufs=8)
-                if half == 1 and j % 2 == 1:
-                    nc.scalar.activation(out=result[:], in_=sums[j][:], func=ACT.Identity, bias=bias_sb[:, j : j + 1])
+                if half == 0 or j % 2 == 1:
+                    nc.scalar.activation(out=result[:], in_=sums[half][j][:], func=ACT.Identity, bias=bias_sb[:, j : j + 1])
                 else:
-                    nc.vector.tensor_scalar_add(out=result[:], in0=sums[j][:], scalar1=bias_sb[:, j : j + 1])
+                    nc.vector.tensor_scalar_add(out=result[:], in0=sums[half][j][:], scalar1=bias_sb[:, j : j + 1])
                 nc.sync.dma_start(out=out[j * P : (j + 1) * P, cols], in_=result[:])

from contextlib import ExitStack

import concourse.mybir as mybir

K, T, S, M, H, N = 1536, 2048, 1024, 512, 1024, 512
FLOPS = 2 * K * H * S + 2 * 2 * H * N * M

F32 = mybir.dt.float32
BF16 = mybir.dt.bfloat16
I32 = mybir.dt.int32
U32 = mybir.dt.uint32
U16 = mybir.dt.uint16
U8 = mybir.dt.uint8
FP8X4 = mybir.dt.float8_e4m3fn_x4
FP4X4 = mybir.dt.float4_e2m1fn_x4
ACT = mybir.ActivationFunctionType
ALU = mybir.AluOpType

P = 128
PACK = 4
K_PASS = P * PACK
K_PASSES = K // K_PASS
R_PASSES = H // K_PASS
BANK = 512
HALF = M // 2
GPSIMD_W1 = ()
GPSIMD_W4 = False


def tile_list_burst_cancel_scores_kernel(
    tc, tab_words, tab_scales, offs, pos1, pos2, w1, thr, temp, sgn, gain, focus, w4, w5_words, w5_scales, bias, out
):
    nc = tc.nc
    with ExitStack() as ctx:
        lists = ctx.enter_context(tc.tile_pool(name="lists", bufs=1))
        keep = ctx.enter_context(tc.tile_pool(name="keep", bufs=1))
        ring = ctx.enter_context(tc.tile_pool(name="ring", bufs=1))
        psum = ctx.enter_context(tc.psum_pool(name="psum", bufs=1))

        offs_sb = lists.tile([P, S // 16], U16, name="offs_sb")
        pos1_sb = lists.tile([P, M // 16], U16, name="pos1_sb")
        pos2_sb = lists.tile([P, M // 16], U16, name="pos2_sb")

        def load_rows(src, name):
            raw = ring.tile([P, PACK, 512], F32, name=name, tag="raw", bufs=5)
            nc.sync.dma_start(out=raw[:], in_=src.rearrange("(p j) c -> p j c", j=PACK))
            return raw

        def load_table(a):
            words = keep.tile([P, T], I32, name=f"tab{a}")
            nc.sync.dma_start(out=words[:], in_=tab_words[a].rearrange("p t i -> p (t i)").bitcast(I32))
            return words

        def load_vector(vec, name):
            col = keep.tile([P, R_PASSES, PACK], F32, name=name)
            nc.sync.dma_start(out=col[:], in_=vec.rearrange("(b p t) -> p b t", p=P, t=PACK))
            return col[:].rearrange("p b t -> p (b t)")

        def w1_rows(a, b):
            return w1[a * K_PASS : (a + 1) * K_PASS, b * 512 : (b + 1) * 512]

        tab_planes = keep.tile([P, T], U8, name="tab_planes")
        nc.gpsimd.memset(tab_planes[:].bitcast(I32), 0)
        w5_planes = keep.tile([P, R_PASSES, N], U8, name="w5_planes", align_bytes=64)
        nc.gpsimd.memset(w5_planes[:].rearrange("p a n -> p (a n)").bitcast(I32), 0)
        tab = []
        w1_raw = {}
        tab.append(load_table(0))
        nc.sync.dma_start(offs_sb[:], offs)
        w1_raw[0, 0] = load_rows(w1_rows(0, 0), "w1raw00")
        for q in range(4):
            nc.sync.dma_start(
                out=tab_planes[32 * q : 32 * q + 4 * K_PASSES, :].bitcast(I32),
                in_=tab_scales[:, 4 * q : 4 * q + 4, :].bitcast(I32),
            )
        for a in range(1, K_PASSES):
            tab.append(load_table(a))
            if a < K_PASSES - 1:
                w1_raw[a, 0] = load_rows(w1_rows(a, 0), f"w1raw{a}0")
        last_halves = []
        for half in range(2):
            part = keep.tile([P, PACK, 256], F32, name=f"w1last{half}")
            src = w1[(K_PASSES - 1) * K_PASS :, half * 256 : (half + 1) * 256]
            nc.sync.dma_start(out=part[:], in_=src.rearrange("(p j) c -> p j c", j=PACK))
            last_halves.append(part)
        w1_raw[0, 1] = load_rows(w1_rows(0, 1), "w1raw01")
        w1_raw[1, 1] = load_rows(w1_rows(1, 1), "w1raw11")
        w1_raw[2, 1] = load_rows(w1_rows(2, 1), "w1raw21")
        nc.sync.dma_start(pos1_sb[:], pos1)
        thr_sb = load_vector(thr, "thr_sb")
        nc.sync.dma_start(pos2_sb[:], pos2)
        temp_sb = load_vector(temp, "temp_sb")
        gain_sb = load_vector(gain, "gain_sb")
        sgn_sb = load_vector(sgn, "sgn_sb")
        focus_sb = [load_rows(focus[b * K_PASS : (b + 1) * K_PASS, :], f"focus{b}") for b in range(R_PASSES)]
        w4_raw = [load_rows(w4[b * K_PASS : (b + 1) * K_PASS, :], f"w4raw{b}") for b in range(R_PASSES)]
        w5_codes = keep.tile([P, R_PASSES, 2 * N], U8, name="w5_codes", align_bytes=64)
        nc.sync.dma_start(out=w5_codes[:].bitcast(I32), in_=w5_words.rearrange("a p n -> p a n").bitcast(I32))
        for q in range(4):
            nc.sync.dma_start(
                out=w5_planes[32 * q : 32 * q + 4, :, :].bitcast(I32),
                in_=w5_scales[:, 4 * q : 4 * q + 4, :].rearrange("a q n -> q a n").bitcast(I32),
            )
        bias_sb = keep.tile([P, N // P], F32, name="bias_sb")
        with nc.allow_non_contiguous_dma(reason="one bias value for each output row"):
            nc.sync.dma_start(out=bias_sb[:], in_=bias.rearrange("(j p) -> p j", p=P))

        def staging(name):
            return ring.tile([P, 2048], BF16, name=name, tag="bf", bufs=2, align_bytes=64)

        def quantize(grouped, name):
            width = grouped.shape[1] // PACK
            codes = keep.tile([P, width], U32, name=name + "_codes", align_bytes=64)
            planes = keep.tile([P, width], U8, name=name + "_planes", align_bytes=64)
            nc.vector.quantize_mx(out=codes[:].bitcast(FP8X4), scales=planes[:], in_=grouped[:])
            return codes, planes

        def round_w1(a, b):
            if (a, b) == (1, 1):
                grouped = ring.tile([P, 2048], BF16, name="w1bf11", tag="handover", bufs=1, align_bytes=64)
            else:
                grouped = staging(f"w1bf{a}{b}")
            dealt = grouped[:].rearrange("p (t m j) -> p m j t", t=PACK, j=PACK)
            if (a, b) == (K_PASSES - 1, 0):
                nc.scalar.copy(out=dealt[:, 0:64], in_=last_halves[0][:].rearrange("p j (m t) -> p m j t", t=PACK))
                nc.scalar.copy(out=dealt[:, 64:128], in_=last_halves[1][:].rearrange("p j (m t) -> p m j t", t=PACK))
            elif (a, b) == (K_PASSES - 1, 1):
                natural = w1_raw[a, b][:].rearrange("p j (m t) -> p m j t", t=PACK)
                nc.vector.tensor_copy(out=dealt[:, 0:64], in_=natural[:, 0:64])
                nc.scalar.copy(out=dealt[:, 64:128], in_=natural[:, 64:128])
            elif (a, b) in GPSIMD_W1:
                nc.gpsimd.tensor_scalar(
                    out=dealt, in0=w1_raw[a, b][:].rearrange("p j (m t) -> p m j t", t=PACK),
                    scalar1=1.0, scalar2=0.0, op0=ALU.mult, op1=ALU.add,
                )
            else:
                nc.scalar.copy(out=dealt, in_=w1_raw[a, b][:].rearrange("p j (m t) -> p m j t", t=PACK))
            return grouped

        def gather_words(a):
            picked = keep.tile([P, S], U32, name=f"picked{a}", align_bytes=64)
            nc.vector.tensor_copy(picked[:], tab[a][:].bitcast(U32).indirect(offs_sb[:]))
            return picked

        picked_planes = keep.tile([P, S], U8, name="picked_planes", align_bytes=64)
        picked = []
        peaks = keep.tile([P, 2, R_PASSES * PACK], F32, name="peaks")
        h = {}
        w1_q = {}

        def multiply(b):
            banks = {}
            for t in range(PACK):
                for half in range(2):
                    banks[t, half] = psum.tile([P, BANK], F32, name=f"h{b}{t}{half}", tag=f"bank{2 * t + half}")
                for a in range(K_PASSES):
                    codes, planes = w1_q[a, b]
                    for half in range(2):
                        cols = slice(half * BANK, (half + 1) * BANK)
                        nc.tensor.matmul_mx(
                            out=banks[t, half][:],
                            lhsT=codes[:, t * P : (t + 1) * P].bitcast(FP8X4),
                            lhsT_scale=planes[:, t * P : (t + 1) * P],
                            rhs=picked[a][:, cols].bitcast(FP8X4),
                            rhs_scale=picked_planes[4 * a : P, cols],
                            start=(a == 0),
                            stop=(a == K_PASSES - 1),
                        )
            return banks

        def empty(b, banks):
            for t in range(PACK):
                if (b, t) == (0, PACK - 1):
                    h[b, t] = ring.tile([P, S], F32, name="hsb03", tag="handover", bufs=1, align_bytes=64)
                else:
                    h[b, t] = keep.tile([P, S], F32, name=f"hsb{b}{t}")
                for half in range(2):
                    nc.vector.tensor_scalar(
                        out=h[b, t][:, half * BANK : (half + 1) * BANK],
                        in0=banks[t, half][:],
                        scalar1=1.0,
                        scalar2=None,
                        op0=ALU.mult,
                        op1=ALU.max,
                        accum_out=peaks[:, half, PACK * b + t : PACK * b + t + 1],
                    )

        for a in range(K_PASSES):
            picked.append(gather_words(a))
            if a == 0:
                nc.vector.tensor_copy(picked_planes[:], tab_planes[:].indirect(offs_sb[:]))
            w1_q[a, 0] = quantize(round_w1(a, 0), f"w1q{a}0")
        banks = multiply(0)
        for a in range(K_PASSES):
            w1_q[a, 1] = quantize(round_w1(a, 1), f"w1q{a}1")
        empty(0, banks)
        empty(1, multiply(1))

        burst = []
        for b in range(R_PASSES):
            burst.append(keep.tile([P, PACK, M], F32, name=f"burst{b}"))
            for t in range(PACK):
                r = PACK * b + t
                nc.scalar.activation(
                    out=burst[b][:, t, :], in_=h[b, t][:].indirect(pos1_sb[:]), func=ACT.Sigmoid, bias=thr_sb[:, r : r + 1]
                )

        top = keep.tile([P, R_PASSES * PACK], F32, name="top")
        nc.vector.tensor_tensor(out=top[:], in0=peaks[:, 0, :], in1=peaks[:, 1, :], op=ALU.max)
        exp_bias = keep.tile([P, R_PASSES * PACK], F32, name="exp_bias")
        nc.vector.scalar_tensor_tensor(out=exp_bias[:], in0=top[:], scalar=-1.0, in1=temp_sb, op0=ALU.mult, op1=ALU.mult)
        cancel_gain = keep.tile([P, R_PASSES * PACK], F32, name="cancel_gain")
        nc.vector.scalar_tensor_tensor(out=cancel_gain[:], in0=sgn_sb, scalar=-1.0, in1=gain_sb, op0=ALU.mult, op1=ALU.mult)

        w4_q = []
        for b in range(R_PASSES):
            for t in range(PACK):
                nc.vector.tensor_tensor(out=focus_sb[b][:, t, :], in0=burst[b][:, t, :], in1=focus_sb[b][:, t, :], op=ALU.mult)
            for t in range(PACK):
                r = PACK * b + t
                nc.vector.tensor_scalar_mul(out=burst[b][:, t, :], in0=burst[b][:, t, :], scalar1=gain_sb[:, r : r + 1])

        def prepare_w4(b):
            grouped = staging(f"w4bf{b}")
            w4_out = grouped[:].rearrange("p (c i j) -> p c j i", i=4, j=PACK)
            w4_in = w4_raw[b][:].rearrange("p j (c i) -> p c j i", i=4)
            if GPSIMD_W4:
                nc.gpsimd.tensor_scalar(out=w4_out, in0=w4_in, scalar1=1.0, scalar2=0.0, op0=ALU.mult, op1=ALU.add)
            else:
                nc.vector.tensor_copy(out=w4_out, in_=w4_in)
            w4_q.append(quantize(grouped, f"w4q{b}"))

        for b in range(R_PASSES):
            prepare_w4(b)

        def walk(planes):
            return planes.rearrange("p t (c i) -> p c t i", i=4)

        def weave(grouped):
            return grouped[:].rearrange("p (c i t) -> p c t i", i=4, t=PACK)

        sums = []
        for half in range(2):
            cols = slice(half * HALF, (half + 1) * HALF)
            sums.append([psum.tile([P, HALF], F32, name=f"y{j}{half}", tag=f"bank{2 * j + half}") for j in range(N // P)])
            for b in range(R_PASSES):
                cancel = ring.tile([P, PACK, HALF], F32, name=f"cancel{b}{half}", tag="cancel", bufs=4)
                share = ring.tile([P, PACK, HALF], F32, name=f"share{b}{half}", tag="share", bufs=4)
                for t in range(PACK):
                    r = PACK * b + t
                    nc.scalar.activation(
                        out=cancel[:, t, :],
                        in_=h[b, t][:].indirect(pos2_sb[:, half * (HALF // 16) : (half + 1) * (HALF // 16)]),
                        func=ACT.Exp,
                        bias=exp_bias[:, r : r + 1],
                        scale=temp_sb[:, r : r + 1],
                    )
                for t in range(PACK):
                    r = PACK * b + t
                    nc.scalar.activation(out=share[:, t, :], in_=cancel[:, t, :], func=ACT.Copy, scale=cancel_gain[:, r : r + 1])
                last = half == 1 and b == R_PASSES - 1
                width = HALF // 2 if last else HALF
                pieces = range(0, HALF, width)
                for first, second, op, name in ((cancel, focus_sb[b], ALU.mult, "both"), (share, burst[b], ALU.add, "diff")):
                    for c0 in pieces:
                        feat = ring.tile([P, PACK * width], BF16, name=f"{name}{b}{half}{c0}", tag="feat", bufs=4, align_bytes=64)
                        wide = slice(half * HALF + c0, half * HALF + c0 + width)
                        nc.vector.tensor_tensor(
                            out=weave(feat), in0=walk(first[:, :, c0 : c0 + width]), in1=walk(second[:, :, wide]), op=op
                        )
                        codes, planes = quantize(feat, f"{name}q{b}{half}{c0}")
                        for j in range(N // P):
                            if name == "both":
                                weight = w5_codes[:, b, 2 * j * P : 2 * (j + 1) * P].bitcast(FP4X4)
                                weight_planes = w5_planes[:, b, j * P : (j + 1) * P]
                            else:
                                weight = w4_q[b][0][:, j * P : (j + 1) * P].bitcast(FP8X4)
                                weight_planes = w4_q[b][1][:, j * P : (j + 1) * P]
                            nc.tensor.matmul_mx(
                                out=sums[half][j][:, c0 : c0 + width],
                                lhsT=weight,
                                lhsT_scale=weight_planes,
                                rhs=codes[:].bitcast(FP8X4),
                                rhs_scale=planes[:],
                                start=(b == 0 and name == "both"),
                                stop=(b == R_PASSES - 1 and name == "diff" and c0 == pieces[-1]),
                            )
        for half in range(2):
            cols = slice(half * HALF, (half + 1) * HALF)
            for j in range(N // P):
                result = ring.tile([P, HALF], F32, name=f"out{j}{half}", tag="result", bufs=8)
                if half == 0 or j % 2 == 1:
                    nc.scalar.activation(out=result[:], in_=sums[half][j][:], func=ACT.Identity, bias=bias_sb[:, j : j + 1])
                else:
                    nc.vector.tensor_scalar_add(out=result[:], in0=sums[half][j][:], scalar1=bias_sb[:, j : j + 1])
                nc.sync.dma_start(out=out[j * P : (j + 1) * P, cols], in_=result[:])
